import numpy as np
import ml_dtypes


def mxq(x, axis, fmt="e4m3"):
    dtype, down = {"e4m3": (ml_dtypes.float8_e4m3fn, 7), "e5m2": (ml_dtypes.float8_e5m2, 14)}[fmt]
    v = np.moveaxis(np.asarray(x, np.float32).astype(ml_dtypes.bfloat16).astype(np.float64), axis, -1)
    blocks = v.reshape(v.shape[:-1] + (-1, 32))
    amax = np.abs(blocks).max(-1, keepdims=True)
    byte = np.maximum(np.where(amax > 0, np.frexp(amax)[1] - 1 + 127, 0) - down, 1)
    scale = np.exp2(byte - 127.0)
    codes = (blocks / scale).astype(np.float32).astype(dtype).astype(np.float64)
    return np.moveaxis((codes * scale).reshape(v.shape), -1, axis)


WIDE = False


def mx_kscale(k):
    if not WIDE:
        return np.ones(k)
    levels = np.array([10, -10, 5, -5, 0])
    if k % 512:
        return np.exp2(np.random.permutation(np.resize(levels, k // 32))).repeat(32)
    a = np.empty((k // 512, 16))
    for p in range(k // 512):
        a[p, :8] = np.random.permutation(np.resize(levels, 8))
        for g in range(8):
            far = levels[np.abs(levels - a[p, g]) >= 10]
            a[p, g + 8] = far[np.random.randint(len(far))]
    return np.exp2(a.ravel()).repeat(32)


BF16 = ml_dtypes.bfloat16


def bf(x):
    return np.asarray(x, np.float32).astype(BF16)


def f64(x):
    return np.asarray(x).astype(np.float64)


E2M1 = np.array([0.0, 0.5, 1.0, 1.5, 2.0, 3.0, 4.0, 6.0, -0.0, -0.5, -1.0, -1.5, -2.0, -3.0, -4.0, -6.0])


def pack_weight(w, fmt):
    k, n = w.shape
    w = f64(bf(w)).reshape(k // 32, 32, n)
    amax = np.abs(w).max(1)
    if fmt == "e4m3":
        byte = np.frexp(amax)[1] - 1 + 127 - 7
    else:
        mant, ex = np.frexp(amax / 6.0)
        byte = np.where(mant > 0.5, ex, ex - 1) + 127
    byte = np.clip(np.where(amax > 0, byte, 1), 1, 254)
    scaled = (w * np.exp2(127.0 - byte)[:, None, :]).reshape(k, n).astype(np.float32)
    by_word = np.ascontiguousarray(scaled.reshape(k // 512, 128, 4, n).transpose(0, 1, 3, 2))
    if fmt == "e4m3":
        words = by_word.astype(ml_dtypes.float8_e4m3fn).view(np.uint8)
    else:
        c = by_word.astype(ml_dtypes.float4_e2m1fn).view(np.uint8) & 0xF
        words = c[..., 0::2] | (c[..., 1::2] << 4)
    return np.ascontiguousarray(words), np.ascontiguousarray(byte.astype(np.uint8).reshape(k // 512, 16, n))


def unpack_weight(words, scales, fmt):
    g, p, n, _ = words.shape
    if fmt == "e4m3":
        vals = np.ascontiguousarray(words).view(ml_dtypes.float8_e4m3fn).astype(np.float64)
    else:
        nib = np.empty((g, p, n, 4), np.uint8)
        nib[..., 0::2] = words & 0xF
        nib[..., 1::2] = words >> 4
        vals = E2M1[nib]
    vals = vals * np.repeat(np.exp2(scales.astype(np.float64) - 127.0), 8, axis=1)[..., None]
    return vals.transpose(0, 1, 3, 2).reshape(g * 512, n)
def pack4(w):
    words, scales = pack_weight(w, "e2m1")
    return words.reshape(words.shape[0], 128, -1), scales


def unpack4(words, scales):
    return unpack_weight(words.reshape(words.shape[0], 128, -1, 2), scales, "e2m1")


N, D, F = 512, 1024, 1024


def logistic(g):
    return 1.0 / (1.0 + np.exp(-g))


def draw0():
    s, t = mx_kscale(D), mx_kscale(F)
    x = bf(np.random.standard_normal((N, D)) * s)
    dx = bf(np.random.standard_normal((N, D)) * s)
    wg_words, wg_scales = pack4(np.random.standard_normal((D, F)) / np.sqrt(D) / s[:, None])
    wu_words, wu_scales = pack4(np.random.standard_normal((D, F)) / np.sqrt(D) / s[:, None] * t)
    wd_words, wd_scales = pack4(np.random.standard_normal((F, D)) / np.sqrt(F) / t[:, None])
    return {"x": x,
            "dx": dx,
            "wg_words": wg_words, "wg_scales": wg_scales,
            "wu_words": wu_words, "wu_scales": wu_scales,
            "wd_words": wd_words, "wd_scales": wd_scales}


def core(x, dx, wg_words, wg_scales, wu_words, wu_scales, wd_words, wd_scales):
    xq = mxq(f64(x), 1, "e4m3")
    dxq = mxq(f64(dx), 1, "e4m3")
    wgq = unpack4(wg_words, wg_scales)
    wuq = unpack4(wu_words, wu_scales)
    g = xq @ wgq
    dg = dxq @ wgq
    u = xq @ wuq
    du = dxq @ wuq
    s = logistic(g)
    sp = s * (1.0 + g * (1.0 - s))
    dh = sp * dg * u + g * s * du
    return mxq(dh, 1, "e4m3") @ unpack4(wd_words, wd_scales)


def e4m3fn_bytes(y):
    return np.clip(np.asarray(y, np.float64), -448.0, 448.0).astype(np.float32).astype(ml_dtypes.float8_e4m3fn).view(np.uint8)


def e4m3fn_values(b):
    return np.asarray(b, np.uint8).view(ml_dtypes.float8_e4m3fn).astype(np.float64)


def setup_inputs():
    d = draw0()
    x0 = np.asarray(d['x']).astype(np.float64)
    s = (np.max(np.abs(x0), axis=(0,), keepdims=True) / 448.0).astype(np.float32)
    out = {}
    for k, v in d.items():
        if k == 'x':
            out['x_bytes'] = e4m3fn_bytes(x0 / s.astype(np.float64))
            out['x_scale'] = s
        else:
            out[k] = v
    return out


def reference(x_bytes, x_scale, dx, wg_words, wg_scales, wu_words, wu_scales, wd_words, wd_scales):
    return core(e4m3fn_values(x_bytes) * x_scale.astype(np.float64), dx, wg_words, wg_scales, wu_words, wu_scales, wd_words, wd_scales)

@@ -1,0 +1,281 @@
+from contextlib import ExitStack
+
+import concourse.mybir as mybir
+from concourse.masks import make_identity
+
+TOKENS, D, F = 512, 1024, 1024
+FLOPS = 5 * 2 * TOKENS * D * F
+
+F32 = mybir.dt.float32
+BF16 = mybir.dt.bfloat16
+I32 = mybir.dt.int32
+U32 = mybir.dt.uint32
+U8 = mybir.dt.uint8
+FP8 = mybir.dt.float8_e4m3fn
+FP8X4 = mybir.dt.float8_e4m3fn_x4
+FP4X4 = mybir.dt.float4_e2m1fn_x4
+ACT = mybir.ActivationFunctionType
+ALU = mybir.AluOpType
+
+P = 128
+PASS = 512
+PASSES = 2
+HALF = 512
+TILES = TOKENS // P
+UNITS = 2 * TILES
+DEPTH = 2
+
+
+def tile_swigluforwardtangentjvp_w4_kernel(
+    tc, x_bytes, x_scale, dx, wg_words, wg_scales, wu_words, wu_scales, wd_words, wd_scales, out
+):
+    nc = tc.nc
+    with ExitStack() as ctx:
+        sb = ctx.enter_context(tc.tile_pool(name="sb", bufs=1))
+        ps = ctx.enter_context(tc.psum_pool(name="ps", bufs=1))
+        ctx.enter_context(tc.manual_schedule())
+
+        def tiles(label, count, shape, dtype):
+            return [sb.tile(shape, dtype, name="%s%d" % (label, j), align_bytes=64) for j in range(count)]
+
+        bank_g, bank_dg, bank_u, bank_du, bank_a, bank_b, bank_c, bank_o = [
+            ps.tile([P, HALF], F32, name="bank%d" % j) for j in range(8)
+        ]
+        bank_gate = [bank_g, bank_o]
+        ident = sb.tile([P, P], F32, name="ident", align_bytes=64)
+        scale_x = sb.tile([P, PASSES, 4], F32, name="scale_x", align_bytes=64)
+        raw_x = tiles("raw_x", TILES // 2, [P, 2, D], U8)
+        wide_x = tiles("wide_x", TILES * PASSES, [P, PASS], BF16)
+        rows_dx = tiles("rows_dx", TILES, [P, D], BF16)
+        words = {w: tiles("words_" + w, 2, [P, PASSES, 2 * HALF], U8) for w in "gud"}
+        planes = {w: sb.tile([P, PASSES, F], U8, name="plane_" + w, align_bytes=64) for w in "gud"}
+        hbm_words = {"g": wg_words, "u": wu_words, "d": wd_words}
+        hbm_scales = {"g": wg_scales, "u": wu_scales, "d": wd_scales}
+        turned = {a: tiles("turned_" + a, TILES, [P, D], BF16) for a in ("x", "dx", "dh")}
+        codes = {a: tiles("codes_" + a, TILES, [P, PASSES * P], U32) for a in ("x", "dx", "dh")}
+        scales = {a: tiles("scales_" + a, TILES, [P, PASSES * P], U8) for a in ("x", "dx", "dh")}
+        silu_neg, tanh_half, silu_pos, p1, p2, p3, p4 = [
+            tiles(label, DEPTH, [P, HALF], F32) for label in ("silu_neg", "tanh_half", "silu_pos", "pa", "pb", "pc", "pd")
+        ]
+        rows_dh = tiles("rows_dh", UNITS, [P, HALF], BF16)
+        result = tiles("result", UNITS, [P, HALF], F32)
+
+        def load_rows(dst, src, i):
+            nc.sync.dma_start(out=dst[i][:], in_=src[i * P : (i + 1) * P, :])
+
+        def load_x(j):
+            src = x_bytes[2 * P * j : 2 * P * (j + 1), :].rearrange("(i p) k -> p i k", p=P)
+            nc.sync.dma_start(out=raw_x[j][:], in_=src)
+
+        def load_words(w, h):
+            src = hbm_words[w].rearrange("g p n -> p g n")[:, :, 2 * HALF * h : 2 * HALF * (h + 1)]
+            nc.sync.dma_start(out=words[w][h][:].bitcast(I32), in_=src.bitcast(I32))
+
+        def load_scales(w):
+            for q in range(4):
+                src = hbm_scales[w][:, 4 * q : 4 * q + 4, :].rearrange("g r n -> r g n")
+                nc.sync.dma_start(out=planes[w][32 * q : 32 * q + 4, :, :].bitcast(I32), in_=src.bitcast(I32))
+
+        def widen(i, g, cast):
+            cast(out=wide_x[PASSES * i + g][:], in_=raw_x[i // 2][:, i % 2, PASS * g : PASS * (g + 1)].bitcast(FP8))
+
+        def turn(bank, g, rows):
+            pairs = rows.bitcast(F32)
+            for u in range(2):
+                col = P * (2 * g + u)
+                nc.tensor.transpose(bank[:, col : col + P], pairs[:, u : 2 * P : 2], ident[:])
+
+        def turn_x(bank, i):
+            for g in range(PASSES):
+                turn(bank, g, wide_x[PASSES * i + g][:])
+
+        def turn_dx(bank, i):
+            for g in range(PASSES):
+                turn(bank, g, rows_dx[i][:, PASS * g : PASS * (g + 1)])
+
+        def scale_out_x(bank, i, g):
+            src = bank[:, 2 * P * g : 2 * P * (g + 1)].bitcast(BF16).rearrange("p (u r e) -> p r u e", u=2, e=2)
+            dst = turned["x"][i][:, PASS * g : PASS * (g + 1)].rearrange("p (r u e) -> p r u e", u=2, e=2)
+            factor = scale_x[:, g, :].rearrange("p (u e) -> p u e", u=2).unsqueeze(1).to_broadcast([P, P, 2, 2])
+            nc.vector.tensor_tensor(out=dst, in0=src, in1=factor, op=ALU.mult)
+
+        def copy_out(bank, a, i, first, count):
+            src = bank[:, 2 * P * first : 2 * P * (first + count)].rearrange("p (g u r) -> p g r u", u=2, r=P)
+            dst = turned[a][i][:, PASS * first : PASS * (first + count)].bitcast(F32)
+            nc.scalar.copy(out=dst.rearrange("p (g r u) -> p g r u", u=2, r=P), in_=src)
+
+        def quantise(a, i, first, count):
+            cols = slice(P * first, P * (first + count))
+            nc.vector.quantize_mx(
+                out=codes[a][i][:, cols].bitcast(FP8X4),
+                scales=scales[a][i][:, cols],
+                in_=turned[a][i][:, PASS * first : PASS * (first + count)],
+            )
+
+        def mx_pass(bank, a, i, w, h, g):
+            cols = slice(P * g, P * (g + 1))
+            nc.tensor.matmul_mx(
+                out=bank[:],
+                lhsT=codes[a][i][:, cols].bitcast(FP8X4),
+                lhsT_scale=scales[a][i][:, cols],
+                rhs=words[w][h][:, g, :].bitcast(FP4X4),
+                rhs_scale=planes[w][:, g, HALF * h : HALF * (h + 1)],
+                start=(g == 0),
+                stop=(g == PASSES - 1),
+            )
+
+        def product(bank, a, i, w, h):
+            for g in range(PASSES):
+                mx_pass(bank, a, i, w, h, g)
+
+        def stage_one(bank, a, w, n):
+            product(bank, a, n // 2, w, n % 2)
+
+        def of_gate(dst, func, scale, n):
+            nc.scalar.activation(out=dst[n % DEPTH][:], in_=bank_gate[n % 2][:], func=func, scale=scale)
+
+        def term_dg(n):
+            s = n % DEPTH
+            nc.vector.scalar_tensor_tensor(
+                out=p1[s][:], in0=silu_neg[s][:], scalar=1.0, in1=bank_dg[:], op0=ALU.subtract, op1=ALU.mult
+            )
+
+        def term_u(n):
+            s = n % DEPTH
+            nc.vector.scalar_tensor_tensor(
+                out=p2[s][:], in0=tanh_half[s][:], scalar=1.0, in1=bank_u[:], op0=ALU.add, op1=ALU.mult
+            )
+
+        def term_du(n):
+            s = n % DEPTH
+            nc.vector.tensor_tensor(out=p3[s][:], in0=silu_pos[s][:], in1=bank_du[:], op=ALU.mult)
+
+        def term_both(n):
+            s = n % DEPTH
+            nc.vector.scalar_tensor_tensor(
+                out=p4[s][:], in0=p1[s][:], scalar=-0.5, in1=p2[s][:], op0=ALU.mult, op1=ALU.mult
+            )
+
+        def finish(n):
+            s = n % DEPTH
+            nc.vector.tensor_tensor(out=rows_dh[n][:], in0=p3[s][:], in1=p4[s][:], op=ALU.add)
+
+        def store(bank, i, h, copy, queue):
+            copy(out=result[2 * i + h][:], in_=bank[:])
+            queue.dma_start(out=out[i * P : (i + 1) * P, HALF * h : HALF * (h + 1)], in_=result[2 * i + h][:])
+
+        for w in "gud":
+            nc.vector.memset(planes[w][:].bitcast(I32), 0)
+        make_identity(nc, ident[:])
+        load_x(0)
+        nc.sync.dma_start(out=scale_x[:], in_=x_scale.rearrange("o (g p t) -> p (o g) t", p=P, t=4))
+        load_rows(rows_dx, dx, 0)
+        load_rows(rows_dx, dx, 1)
+        load_scales("g")
+        load_words("g", 0)
+        load_scales("u")
+        load_words("u", 0)
+        load_words("g", 1)
+        load_x(1)
+        load_rows(rows_dx, dx, 2)
+        load_words("u", 1)
+        load_rows(rows_dx, dx, 3)
+        load_scales("d")
+        load_words("d", 0)
+        load_words("d", 1)
+
+        for g in range(PASSES):
+            widen(0, g, nc.vector.tensor_copy)
+            widen(1, g, nc.scalar.copy)
+        turn(bank_a, 0, wide_x[0][:])
+        turn(bank_du, 1, wide_x[1][:])
+        turn_dx(bank_b, 0)
+        turn_x(bank_c, 1)
+        turn_dx(bank_o, 1)
+        copy_out(bank_b, "dx", 0, 0, 2)
+        copy_out(bank_o, "dx", 1, 0, 2)
+        scale_out_x(bank_a, 0, 0)
+        scale_out_x(bank_du, 0, 1)
+        quantise("x", 0, 0, 1)
+        quantise("dx", 0, 0, 2)
+        quantise("x", 0, 1, 1)
+        scale_out_x(bank_c, 1, 0)
+        scale_out_x(bank_c, 1, 1)
+        quantise("dx", 1, 0, 2)
+        quantise("x", 1, 0, 2)
+        stage_one(bank_g, "x", "g", 0)
+        of_gate(silu_neg, ACT.Silu, -1.0, 0)
+        of_gate(tanh_half, ACT.Tanh, 0.5, 0)
+        of_gate(silu_pos, ACT.Silu, 1.0, 0)
+        widen(2, 0, nc.scalar.copy)
+        widen(2, 1, nc.scalar.copy)
+        stage_one(bank_dg, "dx", "g", 0)
+        stage_one(bank_u, "x", "u", 0)
+        stage_one(bank_du, "dx", "u", 0)
+
+        for n in range(UNITS):
+            i, h = divmod(n, 2)
+            last = n == UNITS - 1
+            ahead = {0: 2, 2: 3}.get(n)
+            term_dg(n)
+            if h == 1 and i > 0:
+                quantise("dh", i - 1, 0, 2)
+            if n > 0:
+                finish(n - 1)
+            if not last:
+                stage_one(bank_gate[(n + 1) % 2], "x", "g", n + 1)
+                of_gate(silu_neg, ACT.Silu, -1.0, n + 1)
+                of_gate(tanh_half, ACT.Tanh, 0.5, n + 1)
+                if n == 0:
+                    turn_dx(bank_b, 2)
+                    turn_x(bank_a, 2)
+                stage_one(bank_dg, "dx", "g", n + 1)
+            if last:
+                turn(bank_c, 0, rows_dh[n - 1][:])
+                copy_out(bank_c, "dh", i, 0, 1)
+            if h == 1 and i > 0:
+                product(bank_a, "dh", i - 1, "d", 0)
+                product(bank_b, "dh", i - 1, "d", 1)
+            if h == 0 and i > 0:
+                if ahead:
+                    turn_x(bank_a, ahead)
+                    turn_dx(bank_b, ahead)
+                turn(bank_c, 0, rows_dh[n - 2][:])
+                turn(bank_c, 1, rows_dh[n - 1][:])
+                copy_out(bank_c, "dh", i - 1, 0, 2)
+            if not last:
+                of_gate(silu_pos, ACT.Silu, 1.0, n + 1)
+            if ahead:
+                copy_out(bank_b, "dx", ahead, 0, 2)
+            if n == 1:
+                for g in range(PASSES):
+                    widen(3, g, nc.scalar.copy)
+            if h == 1 and i > 0:
+                store(bank_a, i - 1, 0, nc.scalar.copy, nc.sync)
+                store(bank_b, i - 1, 1, nc.scalar.copy, nc.sync)
+            term_u(n)
+            term_du(n)
+            if not last:
+                stage_one(bank_u, "x", "u", n + 1)
+                stage_one(bank_du, "dx", "u", n + 1)
+            term_both(n)
+            if ahead:
+                scale_out_x(bank_a, ahead, 0)
+                scale_out_x(bank_a, ahead, 1)
+            if last:
+                quantise("dh", i, 0, 1)
+            if n in (1, 3):
+                quantise("dx", n // 2 + 2, 0, 2)
+                quantise("x", n // 2 + 2, 0, 2)
+
+        i = TILES - 1
+        finish(UNITS - 1)
+        mx_pass(bank_g, "dh", i, "d", 0, 0)
+        mx_pass(bank_dg, "dh", i, "d", 1, 0)
+        turn(bank_c, 1, rows_dh[UNITS - 1][:])
+        copy_out(bank_c, "dh", i, 1, 1)
+        quantise("dh", i, 1, 1)
+        mx_pass(bank_g, "dh", i, "d", 0, 1)
+        mx_pass(bank_dg, "dh", i, "d", 1, 1)
+        store(bank_g, i, 0, nc.scalar.copy, nc.scalar)
+        store(bank_dg, i, 1, nc.vector.tensor_copy, nc.sync)

@@ -43,6 +43,8 @@ def tile_swigluforwardtangentjvp_w4_kernel(
         ]
         bank_gate = [bank_g, bank_o]
         ident = sb.tile([P, P], F32, name="ident", align_bytes=64)
+        warm = sb.tile([P, 8], F32, name="warm", align_bytes=64)
+        zeros = sb.tile([P, HALF], BF16, name="zeros", align_bytes=64)
         scale_x = sb.tile([P, PASSES, 4], F32, name="scale_x", align_bytes=64)
         raw_x = tiles("raw_x", TILES // 2, [P, 2, D], U8)
         wide_x = tiles("wide_x", TILES * PASSES, [P, PASS], BF16)
@@ -160,23 +162,33 @@ def tile_swigluforwardtangentjvp_w4_kernel(
             s = n % DEPTH
             nc.vector.tensor_tensor(out=rows_dh[n][:], in0=p3[s][:], in1=p4[s][:], op=ALU.add)
 
-        def store(bank, i, h, copy, queue):
-            copy(out=result[2 * i + h][:], in_=bank[:])
-            queue.dma_start(out=out[i * P : (i + 1) * P, HALF * h : HALF * (h + 1)], in_=result[2 * i + h][:])
+        def store(bank, i, h, copy, first, width):
+            cols = slice(first, first + width)
+            copy(out=result[2 * i + h][:, cols], in_=bank[:, cols])
+            dst = out[i * P : (i + 1) * P, HALF * h + first : HALF * h + first + width]
+            nc.sync.dma_start(out=dst, in_=result[2 * i + h][:, cols])
 
+        def warm_tensor(count):
+            for j in range(count):
+                nc.tensor.matmul(bank_g[:], lhsT=zeros[:, :P], rhs=zeros[:], start=True, stop=True)
+
+        nc.vector.memset(warm[:], 0.0)
+        nc.scalar.activation(out=warm[:, 4:5], in_=warm[:, 0:1], func=ACT.Silu)
+        nc.vector.memset(zeros[:], 0.0)
+        warm_tensor(5)
         for w in "gud":
             nc.vector.memset(planes[w][:].bitcast(I32), 0)
         make_identity(nc, ident[:])
         load_x(0)
         nc.sync.dma_start(out=scale_x[:], in_=x_scale.rearrange("o (g p t) -> p (o g) t", p=P, t=4))
         load_rows(rows_dx, dx, 0)
-        load_rows(rows_dx, dx, 1)
+        load_x(1)
         load_scales("g")
         load_words("g", 0)
         load_scales("u")
         load_words("u", 0)
         load_words("g", 1)
-        load_x(1)
+        load_rows(rows_dx, dx, 1)
         load_rows(rows_dx, dx, 2)
         load_words("u", 1)
         load_rows(rows_dx, dx, 3)
@@ -190,25 +202,22 @@ def tile_swigluforwardtangentjvp_w4_kernel(
         turn(bank_a, 0, wide_x[0][:])
         turn(bank_du, 1, wide_x[1][:])
         turn_dx(bank_b, 0)
+        warm_tensor(2)
         turn_x(bank_c, 1)
-        turn_dx(bank_o, 1)
         copy_out(bank_b, "dx", 0, 0, 2)
-        copy_out(bank_o, "dx", 1, 0, 2)
         scale_out_x(bank_a, 0, 0)
         scale_out_x(bank_du, 0, 1)
         quantise("x", 0, 0, 1)
-        quantise("dx", 0, 0, 2)
         quantise("x", 0, 1, 1)
+        quantise("dx", 0, 0, 2)
         scale_out_x(bank_c, 1, 0)
         scale_out_x(bank_c, 1, 1)
-        quantise("dx", 1, 0, 2)
-        quantise("x", 1, 0, 2)
+        widen(2, 0, nc.scalar.copy)
+        widen(2, 1, nc.scalar.copy)
         stage_one(bank_g, "x", "g", 0)
         of_gate(silu_neg, ACT.Silu, -1.0, 0)
         of_gate(tanh_half, ACT.Tanh, 0.5, 0)
         of_gate(silu_pos, ACT.Silu, 1.0, 0)
-        widen(2, 0, nc.scalar.copy)
-        widen(2, 1, nc.scalar.copy)
         stage_one(bank_dg, "dx", "g", 0)
         stage_one(bank_u, "x", "u", 0)
         stage_one(bank_du, "dx", "u", 0)
@@ -218,6 +227,8 @@ def tile_swigluforwardtangentjvp_w4_kernel(
             last = n == UNITS - 1
             ahead = {0: 2, 2: 3}.get(n)
             term_dg(n)
+            if n < 2:
+                quantise(("x", "dx")[n], 1, 0, 2)
             if h == 1 and i > 0:
                 quantise("dh", i - 1, 0, 2)
             if n > 0:
@@ -226,10 +237,11 @@ def tile_swigluforwardtangentjvp_w4_kernel(
                 stage_one(bank_gate[(n + 1) % 2], "x", "g", n + 1)
                 of_gate(silu_neg, ACT.Silu, -1.0, n + 1)
                 of_gate(tanh_half, ACT.Tanh, 0.5, n + 1)
-                if n == 0:
-                    turn_dx(bank_b, 2)
-                    turn_x(bank_a, 2)
                 stage_one(bank_dg, "dx", "g", n + 1)
+                if n == 0:
+                    turn_x(bank_a, 2)
+                    turn_dx(bank_c, 1)
+                    turn_dx(bank_b, 2)
             if last:
                 turn(bank_c, 0, rows_dh[n - 1][:])
                 copy_out(bank_c, "dh", i, 0, 1)
@@ -245,14 +257,16 @@ def tile_swigluforwardtangentjvp_w4_kernel(
                 copy_out(bank_c, "dh", i - 1, 0, 2)
             if not last:
                 of_gate(silu_pos, ACT.Silu, 1.0, n + 1)
+            if n == 0:
+                copy_out(bank_c, "dx", 1, 0, 2)
             if ahead:
                 copy_out(bank_b, "dx", ahead, 0, 2)
-            if n == 1:
+            if n == 0:
                 for g in range(PASSES):
                     widen(3, g, nc.scalar.copy)
             if h == 1 and i > 0:
-                store(bank_a, i - 1, 0, nc.scalar.copy, nc.sync)
-                store(bank_b, i - 1, 1, nc.scalar.copy, nc.sync)
+                store(bank_a, i - 1, 0, nc.scalar.copy, 0, HALF)
+                store(bank_b, i - 1, 1, nc.scalar.copy, 0, HALF)
             term_u(n)
             term_du(n)
             if not last:
@@ -277,5 +291,6 @@ def tile_swigluforwardtangentjvp_w4_kernel(
         quantise("dh", i, 1, 1)
         mx_pass(bank_g, "dh", i, "d", 0, 1)
         mx_pass(bank_dg, "dh", i, "d", 1, 1)
-        store(bank_g, i, 0, nc.scalar.copy, nc.scalar)
-        store(bank_dg, i, 1, nc.vector.tensor_copy, nc.sync)
+        for first in (0, HALF // 2):
+            store(bank_g, i, 0, nc.scalar.copy, first, HALF // 2)
+            store(bank_dg, i, 1, nc.vector.tensor_copy, first, HALF // 2)

@@ -148,19 +148,45 @@ def tile_swigluforwardtangentjvp_w4_kernel(
                 out=p2[s][:], in0=tanh_half[s][:], scalar=1.0, in1=bank_u[:], op0=ALU.add, op1=ALU.mult
             )
 
+        def by_parity(values):
+            return values.rearrange("q (p u e) -> q u p e", u=2, e=2)
+
         def term_du(n):
             s = n % DEPTH
-            nc.vector.tensor_tensor(out=p3[s][:], in0=silu_pos[s][:], in1=bank_du[:], op=ALU.mult)
+            dst = p3[s][:].rearrange("q (u p e) -> q u p e", u=2, e=2)
+            nc.vector.tensor_tensor(out=dst, in0=by_parity(silu_pos[s][:]), in1=by_parity(bank_du[:]), op=ALU.mult)
 
-        def term_both(n):
+        def term_both(n, u):
             s = n % DEPTH
             nc.vector.scalar_tensor_tensor(
-                out=p4[s][:], in0=p1[s][:], scalar=-0.5, in1=p2[s][:], op0=ALU.mult, op1=ALU.mult
+                out=p4[s][:, 2 * P * u : 2 * P * (u + 1)].rearrange("q (p e) -> q p e", e=2),
+                in0=by_parity(p1[s][:])[:, u],
+                scalar=-0.5,
+                in1=by_parity(p2[s][:])[:, u],
+                op0=ALU.mult,
+                op1=ALU.mult,
             )
 
-        def finish(n):
+        def finish(n, engine, cols):
             s = n % DEPTH
-            nc.vector.tensor_tensor(out=rows_dh[n][:], in0=p3[s][:], in1=p4[s][:], op=ALU.add)
+            engine.tensor_tensor(out=rows_dh[n][:, cols], in0=p3[s][:, cols], in1=p4[s][:, cols], op=ALU.add)
+
+        def turn_dh(bank, n, u):
+            col = P * (2 * (n % 2) + u)
+            nc.tensor.transpose(bank[:, col : col + P], rows_dh[n][:].bitcast(F32)[:, P * u : P * (u + 1)], ident[:])
+
+        def turn_dh_tile(bank, i):
+            for n in (2 * i, 2 * i + 1):
+                for u in range(2):
+                    turn_dh(bank, n, u)
+
+        def down(i, banks):
+            for h in range(2):
+                product(banks[h], "dh", i, "d", h)
+
+        def store_tile(i, banks, copies):
+            for h in range(2):
+                store(banks[h], i, h, copies[h], 0, HALF)
 
         def store(bank, i, h, copy, first, width):
             cols = slice(first, first + width)
@@ -218,79 +244,84 @@ def tile_swigluforwardtangentjvp_w4_kernel(
         of_gate(silu_neg, ACT.Silu, -1.0, 0)
         of_gate(tanh_half, ACT.Tanh, 0.5, 0)
         of_gate(silu_pos, ACT.Silu, 1.0, 0)
-        stage_one(bank_dg, "dx", "g", 0)
-        stage_one(bank_u, "x", "u", 0)
-        stage_one(bank_du, "dx", "u", 0)
 
+        whole = slice(0, HALF)
+        on_scalar = (nc.scalar.copy, nc.scalar.copy)
         for n in range(UNITS):
-            i, h = divmod(n, 2)
             last = n == UNITS - 1
-            ahead = {0: 2, 2: 3}.get(n)
+            stage_one(bank_dg, "dx", "g", n)
+            stage_one(bank_u, "x", "u", n)
+            stage_one(bank_du, "dx", "u", n)
             term_dg(n)
-            if n < 2:
-                quantise(("x", "dx")[n], 1, 0, 2)
-            if h == 1 and i > 0:
-                quantise("dh", i - 1, 0, 2)
-            if n > 0:
-                finish(n - 1)
-            if not last:
-                stage_one(bank_gate[(n + 1) % 2], "x", "g", n + 1)
-                of_gate(silu_neg, ACT.Silu, -1.0, n + 1)
-                of_gate(tanh_half, ACT.Tanh, 0.5, n + 1)
-                stage_one(bank_dg, "dx", "g", n + 1)
-                if n == 0:
-                    turn_x(bank_a, 2)
-                    turn_dx(bank_c, 1)
-                    turn_dx(bank_b, 2)
-            if last:
-                turn(bank_c, 0, rows_dh[n - 1][:])
-                copy_out(bank_c, "dh", i, 0, 1)
-            if h == 1 and i > 0:
-                product(bank_a, "dh", i - 1, "d", 0)
-                product(bank_b, "dh", i - 1, "d", 1)
-            if h == 0 and i > 0:
-                if ahead:
-                    turn_x(bank_a, ahead)
-                    turn_dx(bank_b, ahead)
-                turn(bank_c, 0, rows_dh[n - 2][:])
-                turn(bank_c, 1, rows_dh[n - 1][:])
-                copy_out(bank_c, "dh", i - 1, 0, 2)
-            if not last:
-                of_gate(silu_pos, ACT.Silu, 1.0, n + 1)
-            if n == 0:
-                copy_out(bank_c, "dx", 1, 0, 2)
-            if ahead:
-                copy_out(bank_b, "dx", ahead, 0, 2)
-            if n == 0:
-                for g in range(PASSES):
-                    widen(3, g, nc.scalar.copy)
-            if h == 1 and i > 0:
-                store(bank_a, i - 1, 0, nc.scalar.copy, 0, HALF)
-                store(bank_b, i - 1, 1, nc.scalar.copy, 0, HALF)
             term_u(n)
             term_du(n)
-            if not last:
-                stage_one(bank_u, "x", "u", n + 1)
-                stage_one(bank_du, "dx", "u", n + 1)
-            term_both(n)
-            if ahead:
-                scale_out_x(bank_a, ahead, 0)
-                scale_out_x(bank_a, ahead, 1)
+            for a, i in {0: [("x", 1)], 1: [("dx", 1), ("x", 2)], 2: [("dx", 2)], 3: [("dh", 0), ("x", 3)], 4: [("dx", 3)], 5: [("dh", 1)]}.get(n, []):
+                quantise(a, i, 0, 2)
             if last:
-                quantise("dh", i, 0, 1)
-            if n in (1, 3):
-                quantise("dx", n // 2 + 2, 0, 2)
-                quantise("x", n // 2 + 2, 0, 2)
+                break
+            term_both(n, 0)
+            term_both(n, 1)
+            finish(n, nc.gpsimd, whole)
+            stage_one(bank_gate[(n + 1) % 2], "x", "g", n + 1)
+            of_gate(silu_neg, ACT.Silu, -1.0, n + 1)
+            of_gate(tanh_half, ACT.Tanh, 0.5, n + 1)
+            of_gate(silu_pos, ACT.Silu, 1.0, n + 1)
+            if n == 0:
+                turn_x(bank_a, 2)
+                turn_dx(bank_b, 1)
+                copy_out(bank_b, "dx", 1, 0, 2)
+                widen(3, 0, nc.scalar.copy)
+                widen(3, 1, nc.scalar.copy)
+                scale_out_x(bank_a, 2, 0)
+                scale_out_x(bank_a, 2, 1)
+            if n == 1:
+                turn_dx(bank_c, 2)
+                copy_out(bank_c, "dx", 2, 0, 2)
+            if n == 2:
+                turn_x(bank_a, 3)
+                turn_dh_tile(bank_b, 0)
+                copy_out(bank_b, "dh", 0, 0, 2)
+                scale_out_x(bank_a, 3, 0)
+                scale_out_x(bank_a, 3, 1)
+            if n == 3:
+                turn_dx(bank_c, 3)
+                copy_out(bank_c, "dx", 3, 0, 2)
+            if n == 4:
+                down(0, (bank_b, bank_a))
+                store_tile(0, (bank_b, bank_a), on_scalar)
+            if n == 4:
+                turn_dh_tile(bank_c, 1)
+                copy_out(bank_c, "dh", 1, 0, 2)
+            if n == 6:
+                product(bank_b, "dh", 1, "d", 0)
+                store(bank_b, 1, 0, nc.scalar.copy, 0, HALF)
+            if n == 6:
+                turn_dh_tile(bank_c, 2)
+                copy_out(bank_c, "dh", 2, 0, 2)
 
-        i = TILES - 1
-        finish(UNITS - 1)
-        mx_pass(bank_g, "dh", i, "d", 0, 0)
-        mx_pass(bank_dg, "dh", i, "d", 1, 0)
-        turn(bank_c, 1, rows_dh[UNITS - 1][:])
+        n, i = UNITS - 1, TILES - 1
+        turn_dh(bank_g, n - 1, 0)
+        turn_dh(bank_g, n - 1, 1)
+        copy_out(bank_g, "dh", i, 0, 1)
+        product(bank_a, "dh", 1, "d", 1)
+        store(bank_a, 1, 1, nc.scalar.copy, 0, HALF)
+        quantise("dh", 2, 0, 2)
+        term_both(n, 0)
+        term_both(n, 1)
+        quantise("dh", i, 0, 1)
+        finish(n, nc.vector, slice(0, 2 * P))
+        finish(n, nc.vector, slice(2 * P, HALF))
+        down(2, (bank_dg, bank_u))
+        turn_dh(bank_c, n, 0)
+        turn_dh(bank_c, n, 1)
+        store(bank_dg, 2, 0, nc.vector.tensor_copy, 0, HALF)
         copy_out(bank_c, "dh", i, 1, 1)
         quantise("dh", i, 1, 1)
-        mx_pass(bank_g, "dh", i, "d", 0, 1)
-        mx_pass(bank_dg, "dh", i, "d", 1, 1)
+        store(bank_u, 2, 1, nc.scalar.copy, 0, HALF)
+        mx_pass(bank_o, "dh", i, "d", 0, 0)
+        mx_pass(bank_du, "dh", i, "d", 1, 0)
+        mx_pass(bank_o, "dh", i, "d", 0, 1)
+        mx_pass(bank_du, "dh", i, "d", 1, 1)
         for first in (0, HALF // 2):
-            store(bank_g, i, 0, nc.scalar.copy, first, HALF // 2)
-            store(bank_dg, i, 1, nc.vector.tensor_copy, first, HALF // 2)
+            store(bank_o, i, 0, nc.scalar.copy, first, HALF // 2)
+            store(bank_du, i, 1, nc.vector.tensor_copy, first, HALF // 2)

@@ -24,6 +24,8 @@ HALF = 512
 TILES = TOKENS // P
 UNITS = 2 * TILES
 DEPTH = 2
+WARM_FIRST = 5
+WARM_SECOND = 2
 
 
 def tile_swigluforwardtangentjvp_w4_kernel(
@@ -38,10 +40,10 @@ def tile_swigluforwardtangentjvp_w4_kernel(
         def tiles(label, count, shape, dtype):
             return [sb.tile(shape, dtype, name="%s%d" % (label, j), align_bytes=64) for j in range(count)]
 
-        bank_g, bank_dg, bank_u, bank_du, bank_a, bank_b, bank_c, bank_o = [
+        bank_g_even, bank_dg, bank_u, bank_du, bank_a, bank_b, bank_c, bank_g_odd = [
             ps.tile([P, HALF], F32, name="bank%d" % j) for j in range(8)
         ]
-        bank_gate = [bank_g, bank_o]
+        bank_g = [bank_g_even, bank_g_odd]
         ident = sb.tile([P, P], F32, name="ident", align_bytes=64)
         warm = sb.tile([P, 8], F32, name="warm", align_bytes=64)
         zeros = sb.tile([P, HALF], BF16, name="zeros", align_bytes=64)
@@ -56,18 +58,19 @@ def tile_swigluforwardtangentjvp_w4_kernel(
         turned = {a: tiles("turned_" + a, TILES, [P, D], BF16) for a in ("x", "dx", "dh")}
         codes = {a: tiles("codes_" + a, TILES, [P, PASSES * P], U32) for a in ("x", "dx", "dh")}
         scales = {a: tiles("scales_" + a, TILES, [P, PASSES * P], U8) for a in ("x", "dx", "dh")}
-        silu_neg, tanh_half, silu_pos, p1, p2, p3, p4 = [
-            tiles(label, DEPTH, [P, HALF], F32) for label in ("silu_neg", "tanh_half", "silu_pos", "pa", "pb", "pc", "pd")
+        silu_neg, tanh_half, silu_pos, with_dg, with_u, with_du, with_both = [
+            tiles(label, DEPTH, [P, HALF], F32)
+            for label in ("silu_neg", "tanh_half", "silu_pos", "with_dg", "with_u", "with_du", "with_both")
         ]
         rows_dh = tiles("rows_dh", UNITS, [P, HALF], BF16)
         result = tiles("result", UNITS, [P, HALF], F32)
 
-        def load_rows(dst, src, i):
-            nc.sync.dma_start(out=dst[i][:], in_=src[i * P : (i + 1) * P, :])
-
         def load_x(j):
             src = x_bytes[2 * P * j : 2 * P * (j + 1), :].rearrange("(i p) k -> p i k", p=P)
             nc.sync.dma_start(out=raw_x[j][:], in_=src)
+
+        def load_dx(i):
+            nc.sync.dma_start(out=rows_dx[i][:], in_=dx[i * P : (i + 1) * P, :])
 
         def load_words(w, h):
             src = hbm_words[w].rearrange("g p n -> p g n")[:, :, 2 * HALF * h : 2 * HALF * (h + 1)]
@@ -78,8 +81,17 @@ def tile_swigluforwardtangentjvp_w4_kernel(
                 src = hbm_scales[w][:, 4 * q : 4 * q + 4, :].rearrange("g r n -> r g n")
                 nc.sync.dma_start(out=planes[w][32 * q : 32 * q + 4, :, :].bitcast(I32), in_=src.bitcast(I32))
 
+        def warm_tensor(count):
+            for j in range(count):
+                nc.tensor.matmul(bank_g_even[:], lhsT=zeros[:, :P], rhs=zeros[:], start=True, stop=True)
+
         def widen(i, g, cast):
-            cast(out=wide_x[PASSES * i + g][:], in_=raw_x[i // 2][:, i % 2, PASS * g : PASS * (g + 1)].bitcast(FP8))
+            raw = raw_x[i // 2][:, i % 2, PASS * g : PASS * (g + 1)]
+            cast(out=wide_x[PASSES * i + g][:], in_=raw.bitcast(FP8))
+
+        def widen_tile(i):
+            for g in range(PASSES):
+                widen(i, g, nc.scalar.copy)
 
         def turn(bank, g, rows):
             pairs = rows.bitcast(F32)
@@ -95,18 +107,32 @@ def tile_swigluforwardtangentjvp_w4_kernel(
             for g in range(PASSES):
                 turn(bank, g, rows_dx[i][:, PASS * g : PASS * (g + 1)])
 
+        def turn_dh(bank, n):
+            pairs = rows_dh[n][:].bitcast(F32)
+            for u in range(2):
+                col = P * (2 * (n % 2) + u)
+                nc.tensor.transpose(bank[:, col : col + P], pairs[:, P * u : P * (u + 1)], ident[:])
+
+        def turn_dh_tile(bank, i):
+            turn_dh(bank, 2 * i)
+            turn_dh(bank, 2 * i + 1)
+
         def scale_out_x(bank, i, g):
             src = bank[:, 2 * P * g : 2 * P * (g + 1)].bitcast(BF16).rearrange("p (u r e) -> p r u e", u=2, e=2)
             dst = turned["x"][i][:, PASS * g : PASS * (g + 1)].rearrange("p (r u e) -> p r u e", u=2, e=2)
             factor = scale_x[:, g, :].rearrange("p (u e) -> p u e", u=2).unsqueeze(1).to_broadcast([P, P, 2, 2])
             nc.vector.tensor_tensor(out=dst, in0=src, in1=factor, op=ALU.mult)
 
-        def copy_out(bank, a, i, first, count):
+        def scale_out_x_tile(bank, i):
+            for g in range(PASSES):
+                scale_out_x(bank, i, g)
+
+        def copy_out(bank, a, i, first=0, count=PASSES):
             src = bank[:, 2 * P * first : 2 * P * (first + count)].rearrange("p (g u r) -> p g r u", u=2, r=P)
             dst = turned[a][i][:, PASS * first : PASS * (first + count)].bitcast(F32)
             nc.scalar.copy(out=dst.rearrange("p (g r u) -> p g r u", u=2, r=P), in_=src)
 
-        def quantise(a, i, first, count):
+        def quantise(a, i, first=0, count=PASSES):
             cols = slice(P * first, P * (first + count))
             nc.vector.quantize_mx(
                 out=codes[a][i][:, cols].bitcast(FP8X4),
@@ -114,113 +140,98 @@ def tile_swigluforwardtangentjvp_w4_kernel(
                 in_=turned[a][i][:, PASS * first : PASS * (first + count)],
             )
 
-        def mx_pass(bank, a, i, w, h, g):
-            cols = slice(P * g, P * (g + 1))
-            nc.tensor.matmul_mx(
-                out=bank[:],
-                lhsT=codes[a][i][:, cols].bitcast(FP8X4),
-                lhsT_scale=scales[a][i][:, cols],
-                rhs=words[w][h][:, g, :].bitcast(FP4X4),
-                rhs_scale=planes[w][:, g, HALF * h : HALF * (h + 1)],
-                start=(g == 0),
-                stop=(g == PASSES - 1),
-            )
-
         def product(bank, a, i, w, h):
             for g in range(PASSES):
-                mx_pass(bank, a, i, w, h, g)
+                cols = slice(P * g, P * (g + 1))
+                nc.tensor.matmul_mx(
+                    out=bank[:],
+                    lhsT=codes[a][i][:, cols].bitcast(FP8X4),
+                    lhsT_scale=scales[a][i][:, cols],
+                    rhs=words[w][h][:, g, :].bitcast(FP4X4),
+                    rhs_scale=planes[w][:, g, HALF * h : HALF * (h + 1)],
+                    start=(g == 0),
+                    stop=(g == PASSES - 1),
+                )
 
-        def stage_one(bank, a, w, n):
-            product(bank, a, n // 2, w, n % 2)
+        def gate(n):
+            bank, s = bank_g[n % 2], n % DEPTH
+            product(bank, "x", n // 2, "g", n % 2)
+            nc.scalar.activation(out=silu_neg[s][:], in_=bank[:], func=ACT.Silu, scale=-1.0)
+            nc.scalar.activation(out=tanh_half[s][:], in_=bank[:], func=ACT.Tanh, scale=0.5)
+            nc.scalar.activation(out=silu_pos[s][:], in_=bank[:], func=ACT.Silu, scale=1.0)
 
-        def of_gate(dst, func, scale, n):
-            nc.scalar.activation(out=dst[n % DEPTH][:], in_=bank_gate[n % 2][:], func=func, scale=scale)
+        def tangents(n):
+            product(bank_dg, "dx", n // 2, "g", n % 2)
+            product(bank_u, "x", n // 2, "u", n % 2)
+            product(bank_du, "dx", n // 2, "u", n % 2)
 
-        def term_dg(n):
-            s = n % DEPTH
-            nc.vector.scalar_tensor_tensor(
-                out=p1[s][:], in0=silu_neg[s][:], scalar=1.0, in1=bank_dg[:], op0=ALU.subtract, op1=ALU.mult
-            )
-
-        def term_u(n):
-            s = n % DEPTH
-            nc.vector.scalar_tensor_tensor(
-                out=p2[s][:], in0=tanh_half[s][:], scalar=1.0, in1=bank_u[:], op0=ALU.add, op1=ALU.mult
-            )
-
-        def by_parity(values):
+        def by_pair(values):
             return values.rearrange("q (p u e) -> q u p e", u=2, e=2)
 
-        def term_du(n):
-            s = n % DEPTH
-            dst = p3[s][:].rearrange("q (u p e) -> q u p e", u=2, e=2)
-            nc.vector.tensor_tensor(out=dst, in0=by_parity(silu_pos[s][:]), in1=by_parity(bank_du[:]), op=ALU.mult)
-
-        def term_both(n, u):
+        def take_dg(n):
             s = n % DEPTH
             nc.vector.scalar_tensor_tensor(
-                out=p4[s][:, 2 * P * u : 2 * P * (u + 1)].rearrange("q (p e) -> q p e", e=2),
-                in0=by_parity(p1[s][:])[:, u],
-                scalar=-0.5,
-                in1=by_parity(p2[s][:])[:, u],
-                op0=ALU.mult,
-                op1=ALU.mult,
+                out=with_dg[s][:], in0=silu_neg[s][:], scalar=1.0, in1=bank_dg[:], op0=ALU.subtract, op1=ALU.mult
             )
+
+        def take_u(n):
+            s = n % DEPTH
+            nc.vector.scalar_tensor_tensor(
+                out=with_u[s][:], in0=tanh_half[s][:], scalar=1.0, in1=bank_u[:], op0=ALU.add, op1=ALU.mult
+            )
+
+        def take_du(n):
+            s = n % DEPTH
+            dst = with_du[s][:].rearrange("q (u p e) -> q u p e", u=2, e=2)
+            nc.vector.tensor_tensor(out=dst, in0=by_pair(silu_pos[s][:]), in1=by_pair(bank_du[:]), op=ALU.mult)
+
+        def join(n):
+            s = n % DEPTH
+            for u in range(2):
+                nc.vector.scalar_tensor_tensor(
+                    out=with_both[s][:, 2 * P * u : 2 * P * (u + 1)].rearrange("q (p e) -> q p e", e=2),
+                    in0=by_pair(with_dg[s][:])[:, u],
+                    scalar=-0.5,
+                    in1=by_pair(with_u[s][:])[:, u],
+                    op0=ALU.mult,
+                    op1=ALU.mult,
+                )
 
         def finish(n, engine, cols):
             s = n % DEPTH
-            engine.tensor_tensor(out=rows_dh[n][:, cols], in0=p3[s][:, cols], in1=p4[s][:, cols], op=ALU.add)
+            first_term, second_term = with_du[s][:, cols], with_both[s][:, cols]
+            engine.tensor_tensor(out=rows_dh[n][:, cols], in0=first_term, in1=second_term, op=ALU.add)
 
-        def turn_dh(bank, n, u):
-            col = P * (2 * (n % 2) + u)
-            nc.tensor.transpose(bank[:, col : col + P], rows_dh[n][:].bitcast(F32)[:, P * u : P * (u + 1)], ident[:])
-
-        def turn_dh_tile(bank, i):
-            for n in (2 * i, 2 * i + 1):
-                for u in range(2):
-                    turn_dh(bank, n, u)
-
-        def down(i, banks):
-            for h in range(2):
-                product(banks[h], "dh", i, "d", h)
-
-        def store_tile(i, banks, copies):
-            for h in range(2):
-                store(banks[h], i, h, copies[h], 0, HALF)
-
-        def store(bank, i, h, copy, first, width):
+        def store(bank, i, h, copy, first=0, width=HALF):
             cols = slice(first, first + width)
             copy(out=result[2 * i + h][:, cols], in_=bank[:, cols])
             dst = out[i * P : (i + 1) * P, HALF * h + first : HALF * h + first + width]
             nc.sync.dma_start(out=dst, in_=result[2 * i + h][:, cols])
 
-        def warm_tensor(count):
-            for j in range(count):
-                nc.tensor.matmul(bank_g[:], lhsT=zeros[:, :P], rhs=zeros[:], start=True, stop=True)
-
         nc.vector.memset(warm[:], 0.0)
         nc.scalar.activation(out=warm[:, 4:5], in_=warm[:, 0:1], func=ACT.Silu)
         nc.vector.memset(zeros[:], 0.0)
-        warm_tensor(5)
+        warm_tensor(WARM_FIRST)
         for w in "gud":
             nc.vector.memset(planes[w][:].bitcast(I32), 0)
         make_identity(nc, ident[:])
+
         load_x(0)
         nc.sync.dma_start(out=scale_x[:], in_=x_scale.rearrange("o (g p t) -> p (o g) t", p=P, t=4))
-        load_rows(rows_dx, dx, 0)
-        load_x(1)
+        load_dx(0)
         load_scales("g")
         load_words("g", 0)
         load_scales("u")
         load_words("u", 0)
+        load_x(1)
         load_words("g", 1)
-        load_rows(rows_dx, dx, 1)
-        load_rows(rows_dx, dx, 2)
+        load_dx(1)
+        load_dx(2)
         load_words("u", 1)
-        load_rows(rows_dx, dx, 3)
-        load_scales("d")
+        load_dx(3)
         load_words("d", 0)
         load_words("d", 1)
+        load_scales("d")
 
         for g in range(PASSES):
             widen(0, g, nc.vector.tensor_copy)
@@ -228,100 +239,99 @@ def tile_swigluforwardtangentjvp_w4_kernel(
         turn(bank_a, 0, wide_x[0][:])
         turn(bank_du, 1, wide_x[1][:])
         turn_dx(bank_b, 0)
-        warm_tensor(2)
+        warm_tensor(WARM_SECOND)
         turn_x(bank_c, 1)
-        copy_out(bank_b, "dx", 0, 0, 2)
+        copy_out(bank_b, "dx", 0)
         scale_out_x(bank_a, 0, 0)
         scale_out_x(bank_du, 0, 1)
         quantise("x", 0, 0, 1)
         quantise("x", 0, 1, 1)
-        quantise("dx", 0, 0, 2)
-        scale_out_x(bank_c, 1, 0)
-        scale_out_x(bank_c, 1, 1)
-        widen(2, 0, nc.scalar.copy)
-        widen(2, 1, nc.scalar.copy)
-        stage_one(bank_g, "x", "g", 0)
-        of_gate(silu_neg, ACT.Silu, -1.0, 0)
-        of_gate(tanh_half, ACT.Tanh, 0.5, 0)
-        of_gate(silu_pos, ACT.Silu, 1.0, 0)
+        quantise("dx", 0)
+        scale_out_x_tile(bank_c, 1)
+        gate(0)
+        widen_tile(2)
 
-        whole = slice(0, HALF)
-        on_scalar = (nc.scalar.copy, nc.scalar.copy)
-        for n in range(UNITS):
-            last = n == UNITS - 1
-            stage_one(bank_dg, "dx", "g", n)
-            stage_one(bank_u, "x", "u", n)
-            stage_one(bank_du, "dx", "u", n)
-            term_dg(n)
-            term_u(n)
-            term_du(n)
-            for a, i in {0: [("x", 1)], 1: [("dx", 1), ("x", 2)], 2: [("dx", 2)], 3: [("dh", 0), ("x", 3)], 4: [("dx", 3)], 5: [("dh", 1)]}.get(n, []):
-                quantise(a, i, 0, 2)
-            if last:
-                break
-            term_both(n, 0)
-            term_both(n, 1)
-            finish(n, nc.gpsimd, whole)
-            stage_one(bank_gate[(n + 1) % 2], "x", "g", n + 1)
-            of_gate(silu_neg, ACT.Silu, -1.0, n + 1)
-            of_gate(tanh_half, ACT.Tanh, 0.5, n + 1)
-            of_gate(silu_pos, ACT.Silu, 1.0, n + 1)
-            if n == 0:
-                turn_x(bank_a, 2)
-                turn_dx(bank_b, 1)
-                copy_out(bank_b, "dx", 1, 0, 2)
-                widen(3, 0, nc.scalar.copy)
-                widen(3, 1, nc.scalar.copy)
-                scale_out_x(bank_a, 2, 0)
-                scale_out_x(bank_a, 2, 1)
+        def after_unit_0():
+            turn_dx(bank_b, 1)
+            turn_x(bank_a, 2)
+            turn_dx(bank_c, 2)
+            copy_out(bank_b, "dx", 1)
+            copy_out(bank_c, "dx", 2)
+            widen_tile(3)
+            scale_out_x_tile(bank_a, 2)
+
+        def after_unit_2():
+            turn_x(bank_a, 3)
+            turn_dx(bank_c, 3)
+            turn_dh_tile(bank_b, 0)
+            copy_out(bank_b, "dh", 0)
+            scale_out_x_tile(bank_a, 3)
+
+        def after_unit_3():
+            copy_out(bank_c, "dx", 3)
+
+        def after_unit_4():
+            product(bank_b, "dh", 0, "d", 0)
+            product(bank_a, "dh", 0, "d", 1)
+            store(bank_b, 0, 0, nc.scalar.copy)
+            store(bank_a, 0, 1, nc.scalar.copy)
+            turn_dh_tile(bank_c, 1)
+            copy_out(bank_c, "dh", 1)
+
+        def after_unit_6():
+            product(bank_b, "dh", 1, "d", 0)
+            store(bank_b, 1, 0, nc.scalar.copy)
+
+        beside = {0: after_unit_0, 2: after_unit_2, 3: after_unit_3, 4: after_unit_4, 6: after_unit_6}
+        to_quantise = {
+            0: [("x", 1)],
+            1: [("x", 2)],
+            2: [("dx", 2)],
+            3: [("dh", 0), ("x", 3)],
+            4: [("dx", 3)],
+            5: [("dh", 1)],
+        }
+
+        last_unit, last_tile = UNITS - 1, TILES - 1
+        for n in range(last_unit):
+            tangents(n)
+            take_dg(n)
             if n == 1:
-                turn_dx(bank_c, 2)
-                copy_out(bank_c, "dx", 2, 0, 2)
-            if n == 2:
-                turn_x(bank_a, 3)
-                turn_dh_tile(bank_b, 0)
-                copy_out(bank_b, "dh", 0, 0, 2)
-                scale_out_x(bank_a, 3, 0)
-                scale_out_x(bank_a, 3, 1)
-            if n == 3:
-                turn_dx(bank_c, 3)
-                copy_out(bank_c, "dx", 3, 0, 2)
-            if n == 4:
-                down(0, (bank_b, bank_a))
-                store_tile(0, (bank_b, bank_a), on_scalar)
-            if n == 4:
-                turn_dh_tile(bank_c, 1)
-                copy_out(bank_c, "dh", 1, 0, 2)
-            if n == 6:
-                product(bank_b, "dh", 1, "d", 0)
-                store(bank_b, 1, 0, nc.scalar.copy, 0, HALF)
-            if n == 6:
-                turn_dh_tile(bank_c, 2)
-                copy_out(bank_c, "dh", 2, 0, 2)
+                quantise("dx", 1)
+            take_u(n)
+            take_du(n)
+            for a, i in to_quantise.get(n, []):
+                quantise(a, i)
+            join(n)
+            finish(n, nc.gpsimd, slice(0, HALF))
+            gate(n + 1)
+            if n in beside:
+                beside[n]()
 
-        n, i = UNITS - 1, TILES - 1
-        turn_dh(bank_g, n - 1, 0)
-        turn_dh(bank_g, n - 1, 1)
-        copy_out(bank_g, "dh", i, 0, 1)
+        tangents(last_unit)
+        take_dg(last_unit)
+        take_u(last_unit)
+        take_du(last_unit)
+        turn_dh_tile(bank_c, 2)
+        turn_dh(bank_g_even, last_unit - 1)
+        copy_out(bank_c, "dh", 2)
+        copy_out(bank_g_even, "dh", last_tile, 0, 1)
         product(bank_a, "dh", 1, "d", 1)
-        store(bank_a, 1, 1, nc.scalar.copy, 0, HALF)
-        quantise("dh", 2, 0, 2)
-        term_both(n, 0)
-        term_both(n, 1)
-        quantise("dh", i, 0, 1)
-        finish(n, nc.vector, slice(0, 2 * P))
-        finish(n, nc.vector, slice(2 * P, HALF))
-        down(2, (bank_dg, bank_u))
-        turn_dh(bank_c, n, 0)
-        turn_dh(bank_c, n, 1)
-        store(bank_dg, 2, 0, nc.vector.tensor_copy, 0, HALF)
-        copy_out(bank_c, "dh", i, 1, 1)
-        quantise("dh", i, 1, 1)
-        store(bank_u, 2, 1, nc.scalar.copy, 0, HALF)
-        mx_pass(bank_o, "dh", i, "d", 0, 0)
-        mx_pass(bank_du, "dh", i, "d", 1, 0)
-        mx_pass(bank_o, "dh", i, "d", 0, 1)
-        mx_pass(bank_du, "dh", i, "d", 1, 1)
+        store(bank_a, 1, 1, nc.scalar.copy)
+        join(last_unit)
+        quantise("dh", 2)
+        finish(last_unit, nc.vector, slice(0, 2 * P))
+        finish(last_unit, nc.vector, slice(2 * P, HALF))
+        quantise("dh", last_tile, 0, 1)
+        product(bank_dg, "dh", 2, "d", 0)
+        turn_dh(bank_c, last_unit)
+        product(bank_u, "dh", 2, "d", 1)
+        store(bank_dg, 2, 0, nc.vector.tensor_copy)
+        copy_out(bank_c, "dh", last_tile, 1, 1)
+        quantise("dh", last_tile, 1, 1)
+        store(bank_u, 2, 1, nc.scalar.copy)
+        product(bank_g_odd, "dh", last_tile, "d", 0)
+        product(bank_du, "dh", last_tile, "d", 1)
         for first in (0, HALF // 2):
-            store(bank_o, i, 0, nc.scalar.copy, first, HALF // 2)
-            store(bank_du, i, 1, nc.vector.tensor_copy, first, HALF // 2)
+            store(bank_g_odd, last_tile, 0, nc.scalar.copy, first, HALF // 2)
+            store(bank_du, last_tile, 1, nc.vector.tensor_copy, first, HALF // 2)

from contextlib import ExitStack

import concourse.mybir as mybir
from concourse.masks import make_identity

TOKENS, D, F = 512, 1024, 1024
FLOPS = 5 * 2 * TOKENS * D * F

F32 = mybir.dt.float32
BF16 = mybir.dt.bfloat16
I32 = mybir.dt.int32
U32 = mybir.dt.uint32
U8 = mybir.dt.uint8
FP8 = mybir.dt.float8_e4m3fn
FP8X4 = mybir.dt.float8_e4m3fn_x4
FP4X4 = mybir.dt.float4_e2m1fn_x4
ACT = mybir.ActivationFunctionType
ALU = mybir.AluOpType

P = 128
PASS = 512
PASSES = 2
HALF = 512
TILES = TOKENS // P
UNITS = 2 * TILES
DEPTH = 2
WARM_FIRST = 5
WARM_SECOND = 2


def tile_swigluforwardtangentjvp_w4_kernel(
    tc, x_bytes, x_scale, dx, wg_words, wg_scales, wu_words, wu_scales, wd_words, wd_scales, out
):
    nc = tc.nc
    with ExitStack() as ctx:
        sb = ctx.enter_context(tc.tile_pool(name="sb", bufs=1))
        ps = ctx.enter_context(tc.psum_pool(name="ps", bufs=1))
        ctx.enter_context(tc.manual_schedule())

        def tiles(label, count, shape, dtype):
            return [sb.tile(shape, dtype, name="%s%d" % (label, j), align_bytes=64) for j in range(count)]

        bank_g_even, bank_dg, bank_u, bank_du, bank_a, bank_b, bank_c, bank_g_odd = [
            ps.tile([P, HALF], F32, name="bank%d" % j) for j in range(8)
        ]
        bank_g = [bank_g_even, bank_g_odd]
        ident = sb.tile([P, P], F32, name="ident", align_bytes=64)
        warm = sb.tile([P, 8], F32, name="warm", align_bytes=64)
        zeros = sb.tile([P, HALF], BF16, name="zeros", align_bytes=64)
        scale_x = sb.tile([P, PASSES, 4], F32, name="scale_x", align_bytes=64)
        raw_x = tiles("raw_x", TILES // 2, [P, 2, D], U8)
        wide_x = tiles("wide_x", TILES * PASSES, [P, PASS], BF16)
        rows_dx = tiles("rows_dx", TILES, [P, D], BF16)
        words = {w: tiles("words_" + w, 2, [P, PASSES, 2 * HALF], U8) for w in "gud"}
        planes = {w: sb.tile([P, PASSES, F], U8, name="plane_" + w, align_bytes=64) for w in "gud"}
        hbm_words = {"g": wg_words, "u": wu_words, "d": wd_words}
        hbm_scales = {"g": wg_scales, "u": wu_scales, "d": wd_scales}
        turned = {a: tiles("turned_" + a, TILES, [P, D], BF16) for a in ("x", "dx", "dh")}
        codes = {a: tiles("codes_" + a, TILES, [P, PASSES * P], U32) for a in ("x", "dx", "dh")}
        scales = {a: tiles("scales_" + a, TILES, [P, PASSES * P], U8) for a in ("x", "dx", "dh")}
        silu_neg, tanh_half, silu_pos, with_dg, with_u, with_du, with_both = [
            tiles(label, DEPTH, [P, HALF], F32)
            for label in ("silu_neg", "tanh_half", "silu_pos", "with_dg", "with_u", "with_du", "with_both")
        ]
        rows_dh = tiles("rows_dh", UNITS, [P, HALF], BF16)
        result = tiles("result", UNITS, [P, HALF], F32)

        def load_x(j):
            src = x_bytes[2 * P * j : 2 * P * (j + 1), :].rearrange("(i p) k -> p i k", p=P)
            nc.sync.dma_start(out=raw_x[j][:], in_=src)

        def load_dx(i):
            nc.sync.dma_start(out=rows_dx[i][:], in_=dx[i * P : (i + 1) * P, :])

        def load_words(w, h):
            src = hbm_words[w].rearrange("g p n -> p g n")[:, :, 2 * HALF * h : 2 * HALF * (h + 1)]
            nc.sync.dma_start(out=words[w][h][:].bitcast(I32), in_=src.bitcast(I32))

        def load_scales(w):
            for q in range(4):
                src = hbm_scales[w][:, 4 * q : 4 * q + 4, :].rearrange("g r n -> r g n")
                nc.sync.dma_start(out=planes[w][32 * q : 32 * q + 4, :, :].bitcast(I32), in_=src.bitcast(I32))

        def warm_tensor(count):
            for j in range(count):
                nc.tensor.matmul(bank_g_even[:], lhsT=zeros[:, :P], rhs=zeros[:], start=True, stop=True)

        def widen(i, g, cast):
            raw = raw_x[i // 2][:, i % 2, PASS * g : PASS * (g + 1)]
            cast(out=wide_x[PASSES * i + g][:], in_=raw.bitcast(FP8))

        def widen_tile(i):
            for g in range(PASSES):
                widen(i, g, nc.scalar.copy)

        def turn(bank, g, rows):
            pairs = rows.bitcast(F32)
            for u in range(2):
                col = P * (2 * g + u)
                nc.tensor.transpose(bank[:, col : col + P], pairs[:, u : 2 * P : 2], ident[:])

        def turn_x(bank, i):
            for g in range(PASSES):
                turn(bank, g, wide_x[PASSES * i + g][:])

        def turn_dx(bank, i):
            for g in range(PASSES):
                turn(bank, g, rows_dx[i][:, PASS * g : PASS * (g + 1)])

        def turn_dh(bank, n):
            pairs = rows_dh[n][:].bitcast(F32)
            for u in range(2):
                col = P * (2 * (n % 2) + u)
                nc.tensor.transpose(bank[:, col : col + P], pairs[:, P * u : P * (u + 1)], ident[:])

        def turn_dh_tile(bank, i):
            turn_dh(bank, 2 * i)
            turn_dh(bank, 2 * i + 1)

        def scale_out_x(bank, i, g):
            src = bank[:, 2 * P * g : 2 * P * (g + 1)].bitcast(BF16).rearrange("p (u r e) -> p r u e", u=2, e=2)
            dst = turned["x"][i][:, PASS * g : PASS * (g + 1)].rearrange("p (r u e) -> p r u e", u=2, e=2)
            factor = scale_x[:, g, :].rearrange("p (u e) -> p u e", u=2).unsqueeze(1).to_broadcast([P, P, 2, 2])
            nc.vector.tensor_tensor(out=dst, in0=src, in1=factor, op=ALU.mult)

        def scale_out_x_tile(bank, i):
            for g in range(PASSES):
                scale_out_x(bank, i, g)

        def copy_out(bank, a, i, first=0, count=PASSES):
            src = bank[:, 2 * P * first : 2 * P * (first + count)].rearrange("p (g u r) -> p g r u", u=2, r=P)
            dst = turned[a][i][:, PASS * first : PASS * (first + count)].bitcast(F32)
            nc.scalar.copy(out=dst.rearrange("p (g r u) -> p g r u", u=2, r=P), in_=src)

        def quantise(a, i, first=0, count=PASSES):
            cols = slice(P * first, P * (first + count))
            nc.vector.quantize_mx(
                out=codes[a][i][:, cols].bitcast(FP8X4),
                scales=scales[a][i][:, cols],
                in_=turned[a][i][:, PASS * first : PASS * (first + count)],
            )

        def product(bank, a, i, w, h):
            for g in range(PASSES):
                cols = slice(P * g, P * (g + 1))
                nc.tensor.matmul_mx(
                    out=bank[:],
                    lhsT=codes[a][i][:, cols].bitcast(FP8X4),
                    lhsT_scale=scales[a][i][:, cols],
                    rhs=words[w][h][:, g, :].bitcast(FP4X4),
                    rhs_scale=planes[w][:, g, HALF * h : HALF * (h + 1)],
                    start=(g == 0),
                    stop=(g == PASSES - 1),
                )

        def gate(n):
            bank, s = bank_g[n % 2], n % DEPTH
            product(bank, "x", n // 2, "g", n % 2)
            nc.scalar.activation(out=silu_neg[s][:], in_=bank[:], func=ACT.Silu, scale=-1.0)
            nc.scalar.activation(out=tanh_half[s][:], in_=bank[:], func=ACT.Tanh, scale=0.5)
            nc.scalar.activation(out=silu_pos[s][:], in_=bank[:], func=ACT.Silu, scale=1.0)

        def tangents(n):
            product(bank_dg, "dx", n // 2, "g", n % 2)
            product(bank_u, "x", n // 2, "u", n % 2)
            product(bank_du, "dx", n // 2, "u", n % 2)

        def by_pair(values):
            return values.rearrange("q (p u e) -> q u p e", u=2, e=2)

        def take_dg(n):
            s = n % DEPTH
            nc.vector.scalar_tensor_tensor(
                out=with_dg[s][:], in0=silu_neg[s][:], scalar=1.0, in1=bank_dg[:], op0=ALU.subtract, op1=ALU.mult
            )

        def take_u(n):
            s = n % DEPTH
            nc.vector.scalar_tensor_tensor(
                out=with_u[s][:], in0=tanh_half[s][:], scalar=1.0, in1=bank_u[:], op0=ALU.add, op1=ALU.mult
            )

        def take_du(n):
            s = n % DEPTH
            dst = with_du[s][:].rearrange("q (u p e) -> q u p e", u=2, e=2)
            nc.vector.tensor_tensor(out=dst, in0=by_pair(silu_pos[s][:]), in1=by_pair(bank_du[:]), op=ALU.mult)

        def join(n):
            s = n % DEPTH
            for u in range(2):
                nc.vector.scalar_tensor_tensor(
                    out=with_both[s][:, 2 * P * u : 2 * P * (u + 1)].rearrange("q (p e) -> q p e", e=2),
                    in0=by_pair(with_dg[s][:])[:, u],
                    scalar=-0.5,
                    in1=by_pair(with_u[s][:])[:, u],
                    op0=ALU.mult,
                    op1=ALU.mult,
                )

        def finish(n, engine, cols):
            s = n % DEPTH
            first_term, second_term = with_du[s][:, cols], with_both[s][:, cols]
            engine.tensor_tensor(out=rows_dh[n][:, cols], in0=first_term, in1=second_term, op=ALU.add)

        def store(bank, i, h, copy, first=0, width=HALF):
            cols = slice(first, first + width)
            copy(out=result[2 * i + h][:, cols], in_=bank[:, cols])
            dst = out[i * P : (i + 1) * P, HALF * h + first : HALF * h + first + width]
            nc.sync.dma_start(out=dst, in_=result[2 * i + h][:, cols])

        nc.vector.memset(warm[:], 0.0)
        nc.scalar.activation(out=warm[:, 4:5], in_=warm[:, 0:1], func=ACT.Silu)
        nc.vector.memset(zeros[:], 0.0)
        warm_tensor(WARM_FIRST)
        for w in "gud":
            nc.vector.memset(planes[w][:].bitcast(I32), 0)
        make_identity(nc, ident[:])

        load_x(0)
        nc.sync.dma_start(out=scale_x[:], in_=x_scale.rearrange("o (g p t) -> p (o g) t", p=P, t=4))
        load_dx(0)
        load_scales("g")
        load_words("g", 0)
        load_scales("u")
        load_words("u", 0)
        load_x(1)
        load_words("g", 1)
        load_dx(1)
        load_dx(2)
        load_words("u", 1)
        load_dx(3)
        load_words("d", 0)
        load_words("d", 1)
        load_scales("d")

        for g in range(PASSES):
            widen(0, g, nc.vector.tensor_copy)
            widen(1, g, nc.scalar.copy)
        turn(bank_a, 0, wide_x[0][:])
        turn(bank_du, 1, wide_x[1][:])
        turn_dx(bank_b, 0)
        warm_tensor(WARM_SECOND)
        turn_x(bank_c, 1)
        copy_out(bank_b, "dx", 0)
        scale_out_x(bank_a, 0, 0)
        scale_out_x(bank_du, 0, 1)
        quantise("x", 0, 0, 1)
        quantise("x", 0, 1, 1)
        quantise("dx", 0)
        scale_out_x_tile(bank_c, 1)
        gate(0)
        widen_tile(2)

        def after_unit_0():
            turn_dx(bank_b, 1)
            turn_x(bank_a, 2)
            turn_dx(bank_c, 2)
            copy_out(bank_b, "dx", 1)
            copy_out(bank_c, "dx", 2)
            widen_tile(3)
            scale_out_x_tile(bank_a, 2)

        def after_unit_2():
            turn_x(bank_a, 3)
            turn_dx(bank_c, 3)
            turn_dh_tile(bank_b, 0)
            copy_out(bank_b, "dh", 0)
            scale_out_x_tile(bank_a, 3)

        def after_unit_3():
            copy_out(bank_c, "dx", 3)

        def after_unit_4():
            product(bank_b, "dh", 0, "d", 0)
            product(bank_a, "dh", 0, "d", 1)
            store(bank_b, 0, 0, nc.scalar.copy)
            store(bank_a, 0, 1, nc.scalar.copy)
            turn_dh_tile(bank_c, 1)
            copy_out(bank_c, "dh", 1)

        def after_unit_6():
            product(bank_b, "dh", 1, "d", 0)
            store(bank_b, 1, 0, nc.scalar.copy)

        beside = {0: after_unit_0, 2: after_unit_2, 3: after_unit_3, 4: after_unit_4, 6: after_unit_6}
        to_quantise = {
            0: [("x", 1)],
            1: [("x", 2)],
            2: [("dx", 2)],
            3: [("dh", 0), ("x", 3)],
            4: [("dx", 3)],
            5: [("dh", 1)],
        }

        last_unit, last_tile = UNITS - 1, TILES - 1
        for n in range(last_unit):
            tangents(n)
            take_dg(n)
            if n == 1:
                quantise("dx", 1)
            take_u(n)
            take_du(n)
            for a, i in to_quantise.get(n, []):
                quantise(a, i)
            join(n)
            finish(n, nc.gpsimd, slice(0, HALF))
            gate(n + 1)
            if n in beside:
                beside[n]()

        tangents(last_unit)
        take_dg(last_unit)
        take_u(last_unit)
        take_du(last_unit)
        turn_dh_tile(bank_c, 2)
        turn_dh(bank_g_even, last_unit - 1)
        copy_out(bank_c, "dh", 2)
        copy_out(bank_g_even, "dh", last_tile, 0, 1)
        product(bank_a, "dh", 1, "d", 1)
        store(bank_a, 1, 1, nc.scalar.copy)
        join(last_unit)
        quantise("dh", 2)
        finish(last_unit, nc.vector, slice(0, 2 * P))
        finish(last_unit, nc.vector, slice(2 * P, HALF))
        quantise("dh", last_tile, 0, 1)
        product(bank_dg, "dh", 2, "d", 0)
        turn_dh(bank_c, last_unit)
        product(bank_u, "dh", 2, "d", 1)
        store(bank_dg, 2, 0, nc.vector.tensor_copy)
        copy_out(bank_c, "dh", last_tile, 1, 1)
        quantise("dh", last_tile, 1, 1)
        store(bank_u, 2, 1, nc.scalar.copy)
        product(bank_g_odd, "dh", last_tile, "d", 0)
        product(bank_du, "dh", last_tile, "d", 1)
        for first in (0, HALF // 2):
            store(bank_g_odd, last_tile, 0, nc.scalar.copy, first, HALF // 2)
            store(bank_du, last_tile, 1, nc.vector.tensor_copy, first, HALF // 2)
